import numpy as np
import ml_dtypes


def mxq(x, axis, fmt="e4m3"):
    dtype, down = {"e4m3": (ml_dtypes.float8_e4m3fn, 7), "e5m2": (ml_dtypes.float8_e5m2, 14)}[fmt]
    v = np.moveaxis(np.asarray(x, np.float32).astype(ml_dtypes.bfloat16).astype(np.float64), axis, -1)
    blocks = v.reshape(v.shape[:-1] + (-1, 32))
    amax = np.abs(blocks).max(-1, keepdims=True)
    byte = np.maximum(np.where(amax > 0, np.frexp(amax)[1] - 1 + 127, 0) - down, 1)
    scale = np.exp2(byte - 127.0)
    codes = (blocks / scale).astype(np.float32).astype(dtype).astype(np.float64)
    return np.moveaxis((codes * scale).reshape(v.shape), -1, axis)


WIDE = False


def mx_kscale(k):
    if not WIDE:
        return np.ones(k)
    levels = np.array([10, -10, 5, -5, 0])
    if k % 512:
        return np.exp2(np.random.permutation(np.resize(levels, k // 32))).repeat(32)
    a = np.empty((k // 512, 16))
    for p in range(k // 512):
        a[p, :8] = np.random.permutation(np.resize(levels, 8))
        for g in range(8):
            far = levels[np.abs(levels - a[p, g]) >= 10]
            a[p, g + 8] = far[np.random.randint(len(far))]
    return np.exp2(a.ravel()).repeat(32)


BF16 = ml_dtypes.bfloat16


def bf(x):
    return np.asarray(x, np.float32).astype(BF16)


def f64(x):
    return np.asarray(x).astype(np.float64)


E2M1 = np.array([0.0, 0.5, 1.0, 1.5, 2.0, 3.0, 4.0, 6.0, -0.0, -0.5, -1.0, -1.5, -2.0, -3.0, -4.0, -6.0])


def pack_weight(w, fmt):
    k, n = w.shape
    w = f64(bf(w)).reshape(k // 32, 32, n)
    amax = np.abs(w).max(1)
    if fmt == "e4m3":
        byte = np.frexp(amax)[1] - 1 + 127 - 7
    else:
        mant, ex = np.frexp(amax / 6.0)
        byte = np.where(mant > 0.5, ex, ex - 1) + 127
    byte = np.clip(np.where(amax > 0, byte, 1), 1, 254)
    scaled = (w * np.exp2(127.0 - byte)[:, None, :]).reshape(k, n).astype(np.float32)
    by_word = np.ascontiguousarray(scaled.reshape(k // 512, 128, 4, n).transpose(0, 1, 3, 2))
    if fmt == "e4m3":
        words = by_word.astype(ml_dtypes.float8_e4m3fn).view(np.uint8)
    else:
        c = by_word.astype(ml_dtypes.float4_e2m1fn).view(np.uint8) & 0xF
        words = c[..., 0::2] | (c[..., 1::2] << 4)
    return np.ascontiguousarray(words), np.ascontiguousarray(byte.astype(np.uint8).reshape(k // 512, 16, n))


def unpack_weight(words, scales, fmt):
    g, p, n, _ = words.shape
    if fmt == "e4m3":
        vals = np.ascontiguousarray(words).view(ml_dtypes.float8_e4m3fn).astype(np.float64)
    else:
        nib = np.empty((g, p, n, 4), np.uint8)
        nib[..., 0::2] = words & 0xF
        nib[..., 1::2] = words >> 4
        vals = E2M1[nib]
    vals = vals * np.repeat(np.exp2(scales.astype(np.float64) - 127.0), 8, axis=1)[..., None]
    return vals.transpose(0, 1, 3, 2).reshape(g * 512, n)
def pack4(w):
    words, scales = pack_weight(w, "e2m1")
    return words.reshape(words.shape[0], 128, -1), scales


def unpack4(words, scales):
    return unpack_weight(words.reshape(words.shape[0], 128, -1, 2), scales, "e2m1")


def planes(Y):
    n, m = Y.shape
    b = f64(bf(Y)).reshape(n // 32, 32, m)
    amax = np.abs(b).max(1)
    byte = np.clip(np.where(amax > 0, np.frexp(amax)[1] - 1 + 127 - 7, 1), 1, 254)
    codes = (b * np.exp2(127.0 - byte)[:, None, :]).reshape(n, m).astype(np.float32).astype(ml_dtypes.float8_e4m3fn).view(np.uint8)
    words = codes.reshape(n // 512, 128, 4, m).transpose(0, 1, 3, 2)
    return np.ascontiguousarray(words), np.ascontiguousarray(byte.astype(np.uint8).reshape(n // 512, 16, m))


NS, NT, NA, NB, NQ = 1024, 2048, 512, 1024, 8

HARD = 2.5
HALF_PI = np.pi / 2


def setup_inputs():
    s = mx_kscale(NS)
    t = mx_kscale(NT)
    x = 0.5 * np.random.randn(NS, NT)
    for _ in range(NQ):
        x = x + np.random.randn(NS, 1) * np.random.randn(1, NT) / np.sqrt(NQ)
    wa = HARD * np.random.randn(NS, NA) / np.sqrt(NS)
    wb = HARD * np.random.randn(NS, NB) / np.sqrt(NS)
    x_words, x_scales = pack_weight(x * s[:, None], "e4m3")
    wa_words, wa_scales = pack4(wa / s[:, None])
    q = np.exp(0.8 * np.random.randn(NT))
    root = np.sqrt(q / q.sum())
    return {
        "x_words": x_words, "x_scales": x_scales,
        "wa_words": wa_words, "wa_scales": wa_scales,
        "wb": bf(wb / s[:, None]),
        "snap_a": bf(root * t), "snap_b": bf(root / t),
        "amp_a": bf(2.0 * np.exp(0.3 * np.random.randn(NA))),
        "amp_b": bf(np.exp(0.8 * np.random.randn(NB))),
    }


def reference(x_words, x_scales, wa_words, wa_scales, wb, snap_a, snap_b, amp_a, amp_b):
    xt = unpack_weight(x_words, x_scales, "e4m3").T
    pa = xt @ unpack4(wa_words, wa_scales)
    pb = xt @ mxq(f64(wb), 0, "e4m3")
    ua = np.tanh(pa) * f64(snap_a)[:, None]
    ub = np.tanh(pb) * f64(snap_b)[:, None]
    r = mxq(ua, 0, "e4m3").T @ mxq(ub, 0, "e4m3")
    y = np.sin(HALF_PI * r) * f64(amp_a)[:, None] * f64(amp_b)[None, :]
    words, scales = planes(y.T)
    return y, words, scales

@@ -1,0 +1,405 @@
+import math
+from contextlib import ExitStack
+
+import concourse.mybir as mybir
+from concourse.masks import make_identity
+
+NS, NT, NA, NB = 1024, 2048, 512, 1024
+FLOPS = 2 * NT * NS * (NA + NB) + 2 * NT * NA * NB
+
+F32 = mybir.dt.float32
+BF16 = mybir.dt.bfloat16
+I32 = mybir.dt.int32
+U8 = mybir.dt.uint8
+FP8X4 = mybir.dt.float8_e4m3fn_x4
+FP4X4 = mybir.dt.float4_e2m1fn_x4
+ACT = mybir.ActivationFunctionType
+MULT = mybir.AluOpType.mult
+
+P = 128
+W = 512
+GP_WORDS = 128
+AMP_ROW = 32
+
+
+def tile_onebit_beam_crosscov_k4_kernel(
+    tc, x_words, x_scales, wa_words, wa_scales, wb, snap_a, snap_b, amp_a, amp_b, out_0, out_1, out_2
+):
+    nc = tc.nc
+    with ExitStack() as ctx:
+        keep = ctx.enter_context(tc.tile_pool(name="keep", bufs=1))
+        stage = ctx.enter_context(tc.tile_pool(name="stage", bufs=2))
+        ps_one = ctx.enter_context(tc.psum_pool(name="ps_one", bufs=1))
+        ps_gram = ctx.enter_context(tc.psum_pool(name="ps_gram", bufs=2))
+        ps_beam = ctx.enter_context(tc.psum_pool(name="ps_beam", bufs=4))
+        ctx.enter_context(tc.manual_schedule())
+
+        def kept(name, shape, dtype):
+            return keep.tile(shape, dtype, name=name, align_bytes=64)
+
+        x_raw = [kept("x_raw%d" % s, [P, 2, W], I32) for s in range(4)]
+        x_cod = [kept("x_cod%d" % s, [P, 2, W], I32) for s in range(4)]
+        xs_raw = kept("xs_raw", [P, 2, NT // 4], I32)
+        x_scl = [kept("x_scl%d" % s, [P, 2, W], U8) for s in range(4)]
+        wa_cod = kept("wa_cod", [P, 2, 2 * NA], U8)
+        wa_scl = kept("wa_scl", [P, 2, NA], U8)
+        wb_raw = {(g, h): kept("wb_raw%d%d" % (g, h), [P, 4, W], BF16) for g in range(2) for h in range(2)}
+        wb_grp = {(g, h): kept("wb_grp%d%d" % (g, h), [P, W, 4], BF16) for g in range(2) for h in range(2)}
+        wb_cod = {(g, h): kept("wb_cod%d%d" % (g, h), [P, W], I32) for g in range(2) for h in range(2)}
+        wb_scl = {(g, h): kept("wb_scl%d%d" % (g, h), [P, W], U8) for g in range(2) for h in range(2)}
+        u_cod = [kept("u_cod%d" % i, [P, W], I32) for i in range(12)]
+        u_scl = [kept("u_scl%d" % i, [P, W], U8) for i in range(12)]
+        u_ring = kept("u_ring", [P, 4 * (2 * W - GP_WORDS)], BF16)
+        rows_raw = kept("rows_raw", [P, W], BF16)
+        rows_f32 = kept("rows_f32", [P, 4, P], F32)
+        ident = kept("ident", [P, P], F32)
+        warm = kept("warm", [P, 2], F32)
+        fac_sb = kept("fac_sb", [P, AMP_ROW + 4, 4], F32)
+        amp_b_all = kept("amp_b_all", [P, NB], BF16)
+        y_cod = [kept("y_cod%d" % h, [P, NA], I32) for h in range(2)]
+        y_scl = [kept("y_scl%d" % h, [P, NA], U8) for h in range(2)]
+        fac_ps = ps_one.tile([P, P, 4], F32, name="fac_ps")
+
+        nc.vector.memset(xs_raw[:], 0)
+        nc.vector.memset(wa_scl[:].bitcast(I32), 0)
+        nc.vector.memset(warm[:, 0:1], 0.0)
+        nc.vector.memset(rows_f32[:], 0.0)
+        nc.scalar.activation(out=warm[:, 1:2], in_=warm[:, 0:1], func=ACT.Silu)
+
+        x_view = x_words.rearrange("g p n t -> p g (n t)")
+
+        def load_x(s):
+            nc.sync.dma_start(out=x_raw[s][:], in_=x_view[:, :, 4 * W * s : 4 * W * (s + 1)].bitcast(I32))
+
+        def load_wb(g, h):
+            nc.sync.dma_start(
+                out=wb_raw[g, h][:],
+                in_=wb[W * g : W * (g + 1), W * h : W * (h + 1)].rearrange("(p t) n -> p t n", t=4),
+            )
+
+        def load_scale_rows(queue, plane, scales, q):
+            queue.dma_start(
+                out=plane[32 * q : 32 * q + 4, :, :],
+                in_=scales[:, 4 * q : 4 * q + 4, :].rearrange("g r n -> r g n").bitcast(I32),
+            )
+
+        load_x(0)
+        nc.sync.dma_start(out=wa_cod[:].bitcast(I32), in_=wa_words.rearrange("g p n -> p g n").bitcast(I32))
+        for q in range(4):
+            load_scale_rows(nc.sync, xs_raw, x_scales, q)
+        for q in range(4):
+            load_scale_rows(nc.sync, wa_scl[:].bitcast(I32), wa_scales, q)
+        make_identity(nc, ident[:])
+        nc.sync.dma_start(out=rows_raw[0:4, :], in_=snap_a.rearrange("(s n) -> s n", s=4))
+        nc.sync.dma_start(out=rows_raw[4:8, :], in_=snap_b.rearrange("(s n) -> s n", s=4))
+        nc.sync.dma_start(out=rows_raw[AMP_ROW : AMP_ROW + 4, 0:P], in_=amp_a.rearrange("(s n) -> s n", s=4))
+        load_x(1)
+        load_wb(0, 0)
+        load_x(2)
+        load_wb(1, 0)
+        load_x(3)
+        load_wb(0, 1)
+        load_wb(1, 1)
+        nc.sync.dma_start(out=amp_b_all[:], in_=amp_b.partition_broadcast(P))
+
+        def sort_x(s):
+            nc.vector.tensor_copy(
+                out=x_cod[s][:].rearrange("p g (t q r) -> p g t q r", t=4, r=8),
+                in_=x_raw[s][:].rearrange("p g (q t r) -> p g t q r", t=4, r=8),
+            )
+            nc.vector.tensor_copy(
+                out=x_scl[s][:].bitcast(I32).rearrange("p g (t q r) -> p g t q r", t=4, r=2),
+                in_=xs_raw[:, :, P * s : P * (s + 1)].rearrange("p g (q t r) -> p g t q r", t=4, r=2),
+            )
+
+        def sort_rows():
+            nc.vector.tensor_copy(
+                out=rows_f32[0:8, :, :].rearrange("s t (q r) -> s t q r", r=8),
+                in_=rows_raw[0:8, :].rearrange("s (q t r) -> s t q r", t=4, r=8),
+            )
+            nc.vector.tensor_copy(
+                out=rows_f32[AMP_ROW : AMP_ROW + 4, 0, :],
+                in_=rows_raw[AMP_ROW : AMP_ROW + 4, 0:P],
+            )
+
+        def turn_rows():
+            for t in range(4):
+                nc.tensor.transpose(fac_ps[:, :, t], rows_f32[:, t, :], ident[:])
+
+        def group_wb(engine_copy, g, h, c0, c1):
+            engine_copy(
+                out=wb_grp[g, h][:, c0:c1, :].rearrange("p (c i) t -> p c t i", i=4),
+                in_=wb_raw[g, h][:, :, c0:c1].rearrange("p t (c i) -> p c t i", i=4),
+            )
+
+        def quant_wb(g, h):
+            nc.vector.quantize_mx(
+                out=wb_cod[g, h][:].bitcast(FP8X4),
+                scales=wb_scl[g, h][:],
+                in_=wb_grp[g, h][:].rearrange("p c t -> p (c t)"),
+            )
+
+        hard = {}
+
+        def beam_bank(i, b):
+            s = i % 4
+            bank = ps_beam.tile([P, W], F32, name="beam", tag="beam")
+            if i < 4:
+                j = b if i % 2 else (b + 3) % 4
+                for t in range(4):
+                    for g in range(2):
+                        nc.tensor.matmul_mx(
+                            out=bank[:, P * t : P * (t + 1)],
+                            lhsT=x_cod[s][:, g, P * t : P * (t + 1)].bitcast(FP8X4),
+                            lhsT_scale=x_scl[s][:, g, P * t : P * (t + 1)],
+                            rhs=wa_cod[:, g, 2 * P * j : 2 * P * (j + 1)].bitcast(FP4X4),
+                            rhs_scale=wa_scl[:, g, P * j : P * (j + 1)],
+                            start=(g == 0),
+                            stop=(g == 1),
+                        )
+                slot, k = j, 4
+            else:
+                h = i // 4 - 1
+                c = b // 2 if i % 2 else 1 - b // 2
+                u = b % 2
+                for e in range(2):
+                    t = 2 * u + e
+                    for g in range(2):
+                        nc.tensor.matmul_mx(
+                            out=bank[:, 256 * e : 256 * (e + 1)],
+                            lhsT=x_cod[s][:, g, P * t : P * (t + 1)].bitcast(FP8X4),
+                            lhsT_scale=x_scl[s][:, g, P * t : P * (t + 1)],
+                            rhs=wb_cod[g, h][:, 256 * c : 256 * (c + 1)].bitcast(FP8X4),
+                            rhs_scale=wb_scl[g, h][:, 256 * c : 256 * (c + 1)],
+                            start=(g == 0),
+                            stop=(g == 1),
+                        )
+                slot, k = 2 * c + u, 2
+            nc.scalar.activation(
+                out=hard[i][:, W * slot : W * (slot + 1)].rearrange("p (n t) -> p n t", t=k),
+                in_=bank[:].rearrange("p (t n) -> p n t", t=k),
+                func=ACT.Tanh,
+            )
+
+        def weigh(engine, fac, i, w0, w1):
+            row = i % 4 if i < 4 else 4 + i % 4
+            base = (W - GP_WORDS) * (i % 2)
+            n = w1 - w0
+            dst = u_ring[:, 4 * (base + w0) : 4 * (base + w1)]
+            if i < 4:
+                engine.tensor_tensor(
+                    out=dst.rearrange("p (n t) -> p n t", t=4),
+                    in0=hard[i][:, 4 * w0 : 4 * w1].rearrange("p (n t) -> p n t", t=4),
+                    in1=fac[:, row : row + 1, :].to_broadcast([P, n, 4]),
+                    op=MULT,
+                )
+            else:
+                c = w0 // 256
+                engine.tensor_tensor(
+                    out=dst.rearrange("p (n u e) -> p n u e", u=2, e=2),
+                    in0=hard[i][:].rearrange("p (c u n e) -> p c n u e", c=2, u=2, e=2)[
+                        :, c, w0 - 256 * c : w1 - 256 * c, :, :
+                    ],
+                    in1=fac[:, row : row + 1, :].rearrange("p o (u e) -> p o u e", u=2).to_broadcast([P, n, 2, 2]),
+                    op=MULT,
+                )
+
+        def quant_u(i):
+            base = (W - GP_WORDS) * (i % 2)
+            nc.vector.quantize_mx(
+                out=u_cod[i][:].bitcast(FP8X4), scales=u_scl[i][:], in_=u_ring[:, 4 * base : 4 * (base + W)]
+            )
+
+        gram = {}
+
+        def gram_pass(j, h, s, pool=None):
+            if s == 0:
+                if pool is None:
+                    gram[j, h] = ps_gram.tile([P, W], F32, name="gram", tag="gram")
+                else:
+                    gram[j, h] = ps_beam.tile([P, W], F32, name="beam", tag="beam")
+            i = 4 + 4 * h + s
+            nc.tensor.matmul_mx(
+                out=gram[j, h][:],
+                lhsT=u_cod[s][:, P * j : P * (j + 1)].bitcast(FP8X4),
+                lhsT_scale=u_scl[s][:, P * j : P * (j + 1)],
+                rhs=u_cod[i][:].bitcast(FP8X4),
+                rhs_scale=u_scl[i][:],
+                start=(s == 0),
+                stop=(s == 3),
+            )
+
+        sine = {}
+        y_f32 = {}
+        y_bf = {}
+        y_ps = {}
+        y_grp = {}
+
+        def sin_unit(j, h):
+            sine[j, h] = stage.tile([P, W], F32, name="sine", tag="sine", bufs=3)
+            nc.scalar.activation(out=sine[j, h][:], in_=gram[j, h][:], func=ACT.Sin, scale=math.pi / 2)
+
+        def scale_unit(j, h):
+            y_f32[j, h] = stage.tile([P, W], F32, name="y_f32", tag="y_f32", bufs=4)
+            nc.vector.scalar_tensor_tensor(
+                out=y_f32[j, h][:],
+                in0=sine[j, h][:],
+                scalar=fac_sb[:, AMP_ROW + j, 0:1],
+                in1=amp_b_all[:, W * h : W * (h + 1)],
+                op0=MULT,
+                op1=MULT,
+            )
+            nc.sync.dma_start(out=out_0[P * j : P * (j + 1), W * h : W * (h + 1)], in_=y_f32[j, h][:])
+
+        def round_unit(j, h):
+            y_bf[j, h] = stage.tile([P, W], BF16, name="y_bf", tag="y_bf", bufs=4)
+            nc.vector.tensor_copy(
+                out=y_bf[j, h][:].rearrange("a (u p e) -> a u p e", u=2, e=2),
+                in_=y_f32[j, h][:].rearrange("a (p u e) -> a u p e", u=2, e=2),
+            )
+
+        def turn_units(js, h, tail=False):
+            if tail:
+                bank = ps_beam.tile([P, W], F32, name="beam", tag="beam")
+            else:
+                bank = ps_one.tile([P, W], F32, name="turn", tag="turn")
+            y_ps[js, h] = bank
+            for k, j in enumerate(js):
+                words = y_bf[j, h][:].bitcast(F32)
+                for u in range(2):
+                    nc.tensor.transpose(
+                        bank[:, 256 * k + P * u : 256 * k + P * (u + 1)], words[:, P * u : P * (u + 1)], ident[:]
+                    )
+
+        def copy_units(js, h):
+            n = len(js)
+            y_grp[js, h] = stage.tile([P, 2 * W], BF16, name="y_grp", tag="y_grp", bufs=3, align_bytes=64)
+            nc.scalar.copy(
+                out=y_grp[js, h][:, 0 : W * n].bitcast(F32).rearrange("p (k a u) -> p k a u", k=n, u=2),
+                in_=y_ps[js, h][:, 0 : 256 * n].rearrange("p (k u a) -> p k a u", k=n, u=2),
+            )
+
+        def quant_units(js, h):
+            cols = slice(P * js[0], P * (js[-1] + 1))
+            nc.vector.quantize_mx(
+                out=y_cod[h][:, cols].bitcast(FP8X4), scales=y_scl[h][:, cols], in_=y_grp[js, h][:, 0 : W * len(js)]
+            )
+
+        def store_codes(h, c0, c1, queue):
+            queue.dma_start(
+                out=out_1[h].rearrange("p m t -> p (m t)")[:, 4 * c0 : 4 * c1].bitcast(I32), in_=y_cod[h][:, c0:c1]
+            )
+
+        def store_scales(h, q, queue):
+            queue.dma_start(
+                out=out_2[h, 4 * q : 4 * q + 4, :].bitcast(I32), in_=y_scl[h][32 * q : 32 * q + 4, :].bitcast(I32)
+            )
+
+        sort_x(0)
+        for i in range(12):
+            hard[i] = stage.tile([P, 4 * W], F32, name="hard", tag="hard", bufs=3)
+            for b in range(4):
+                beam_bank(i, b)
+                if i == 0 and b == 0:
+                    sort_x(1)
+                if i == 0 and b == 3:
+                    sort_rows()
+                    turn_rows()
+                    nc.vector.tensor_copy(out=fac_sb[:], in_=fac_ps[:, 0 : AMP_ROW + 4, :])
+                if i == 10 and b < 2:
+                    sin_unit(b, 0)
+                if i == 11 and b < 2:
+                    sin_unit(2 + b, 0)
+            if 6 <= i <= 9:
+                gram_pass(0, 0, i - 6)
+                gram_pass(1, 0, i - 6)
+            if i == 10:
+                for j in (2, 3):
+                    for s in range(4):
+                        gram_pass(j, 0, s)
+            if i == 0:
+                group_wb(nc.scalar.copy, 0, 0, 0, W)
+            if i in (1, 2):
+                group_wb(nc.scalar.copy, 1, 0, 256 * (i - 1), 256 * i)
+            if i in (4, 5):
+                group_wb(nc.scalar.copy, 0, 1, 256 * (i - 4), 256 * (i - 3))
+            if i % 2:
+                gp, first, rest = (0, 128), (128, 256), [(256, 512)]
+            else:
+                gp, first, rest = (384, 512), (256, 384), [(0, 256)]
+            if i < 4:
+                if i % 2:
+                    rest = [(256, 384), (384, 512)]
+                else:
+                    first, rest = (0, 128), [(128, 256), (256, 384)]
+            if i == 0:
+                weigh(nc.vector, fac_ps, i, *gp)
+            weigh(nc.vector, fac_ps, i, *first)
+            if i == 1:
+                sort_x(3)
+                quant_wb(0, 0)
+            if i == 3:
+                quant_wb(1, 0)
+            if i in (4, 5):
+                group_wb(nc.vector.tensor_copy, 1, 1, 256 * (i - 4), 256 * (i - 3))
+            if i == 6:
+                quant_wb(0, 1)
+                quant_wb(1, 1)
+            if i == 10:
+                scale_unit(0, 0)
+                scale_unit(1, 0)
+                round_unit(0, 0)
+            if i == 11:
+                round_unit(1, 0)
+                scale_unit(2, 0)
+                turn_units((0, 1), 0)
+                copy_units((0, 1), 0)
+            if i > 0:
+                quant_u(i - 1)
+                weigh(nc.gpsimd, fac_sb, i, *gp)
+            for piece in rest:
+                weigh(nc.vector, fac_ps, i, *piece)
+            if i == 0:
+                sort_x(2)
+
+        for s in range(3):
+            gram_pass(0, 1, s)
+            gram_pass(1, 1, s)
+        for s in range(3):
+            gram_pass(2, 1, s, pool="beam")
+            gram_pass(3, 1, s, pool="beam")
+        scale_unit(3, 0)
+        quant_u(11)
+        for j in range(4):
+            gram_pass(j, 1, 3)
+        round_unit(2, 0)
+        quant_units((0, 1), 0)
+        round_unit(3, 0)
+        sin_unit(0, 1)
+        sin_unit(1, 1)
+        turn_units((2, 3), 0)
+        copy_units((2, 3), 0)
+        scale_unit(0, 1)
+        sin_unit(2, 1)
+        scale_unit(1, 1)
+        sin_unit(3, 1)
+        round_unit(0, 1)
+        quant_units((2, 3), 0)
+        store_codes(0, 0, NA, nc.sync)
+        for q in range(4):
+            store_scales(0, q, nc.sync)
+        round_unit(1, 1)
+        turn_units((0, 1), 1, tail=True)
+        copy_units((0, 1), 1)
+        scale_unit(2, 1)
+        scale_unit(3, 1)
+        round_unit(2, 1)
+        round_unit(3, 1)
+        turn_units((2, 3), 1, tail=True)
+        copy_units((2, 3), 1)
+        quant_units((0, 1), 1)
+        store_codes(1, 0, 256, nc.sync)
+        quant_units((2, 3), 1)
+        store_codes(1, 256, NA, nc.sync)
+        for q in range(4):
+            store_scales(1, q, nc.sync if q < 2 else nc.scalar)

@@ -30,7 +30,7 @@ def tile_onebit_beam_crosscov_k4_kernel(
         keep = ctx.enter_context(tc.tile_pool(name="keep", bufs=1))
         stage = ctx.enter_context(tc.tile_pool(name="stage", bufs=2))
         ps_one = ctx.enter_context(tc.psum_pool(name="ps_one", bufs=1))
-        ps_gram = ctx.enter_context(tc.psum_pool(name="ps_gram", bufs=2))
+        ps_gram = ctx.enter_context(tc.psum_pool(name="ps_gram", bufs=3))
         ps_beam = ctx.enter_context(tc.psum_pool(name="ps_beam", bufs=4))
         ctx.enter_context(tc.manual_schedule())
 
@@ -39,7 +39,7 @@ def tile_onebit_beam_crosscov_k4_kernel(
 
         x_raw = [kept("x_raw%d" % s, [P, 2, W], I32) for s in range(4)]
         x_cod = [kept("x_cod%d" % s, [P, 2, W], I32) for s in range(4)]
-        xs_raw = kept("xs_raw", [P, 2, NT // 4], I32)
+        xs_raw = [kept("xs_raw0", [P, 2, P], I32), kept("xs_raw1", [P, 2, 3 * P], I32)]
         x_scl = [kept("x_scl%d" % s, [P, 2, W], U8) for s in range(4)]
         wa_cod = kept("wa_cod", [P, 2, 2 * NA], U8)
         wa_scl = kept("wa_scl", [P, 2, NA], U8)
@@ -60,9 +60,10 @@ def tile_onebit_beam_crosscov_k4_kernel(
         y_scl = [kept("y_scl%d" % h, [P, NA], U8) for h in range(2)]
         fac_ps = ps_one.tile([P, P, 4], F32, name="fac_ps")
 
-        nc.vector.memset(xs_raw[:], 0)
         nc.vector.memset(wa_scl[:].bitcast(I32), 0)
         nc.vector.memset(warm[:, 0:1], 0.0)
+        nc.vector.memset(xs_raw[0][:], 0)
+        nc.vector.memset(xs_raw[1][:], 0)
         nc.vector.memset(rows_f32[:], 0.0)
         nc.scalar.activation(out=warm[:, 1:2], in_=warm[:, 0:1], func=ACT.Silu)
 
@@ -83,20 +84,26 @@ def tile_onebit_beam_crosscov_k4_kernel(
                 in_=scales[:, 4 * q : 4 * q + 4, :].rearrange("g r n -> r g n").bitcast(I32),
             )
 
+        wa_scl_words = wa_scl[:].bitcast(I32)
+        for q in range(3):
+            load_scale_rows(nc.sync, wa_scl_words, wa_scales, q)
         load_x(0)
         nc.sync.dma_start(out=wa_cod[:].bitcast(I32), in_=wa_words.rearrange("g p n -> p g n").bitcast(I32))
-        for q in range(4):
-            load_scale_rows(nc.sync, xs_raw, x_scales, q)
-        for q in range(4):
-            load_scale_rows(nc.sync, wa_scl[:].bitcast(I32), wa_scales, q)
+        load_scale_rows(nc.sync, xs_raw[0], x_scales[:, :, 0:W], 0)
+        load_scale_rows(nc.sync, xs_raw[0], x_scales[:, :, 0:W], 2)
+        load_wb(0, 0)
+        load_scale_rows(nc.sync, xs_raw[0], x_scales[:, :, 0:W], 1)
+        load_scale_rows(nc.sync, xs_raw[0], x_scales[:, :, 0:W], 3)
+        load_scale_rows(nc.sync, wa_scl_words, wa_scales, 3)
         make_identity(nc, ident[:])
         nc.sync.dma_start(out=rows_raw[0:4, :], in_=snap_a.rearrange("(s n) -> s n", s=4))
         nc.sync.dma_start(out=rows_raw[4:8, :], in_=snap_b.rearrange("(s n) -> s n", s=4))
         nc.sync.dma_start(out=rows_raw[AMP_ROW : AMP_ROW + 4, 0:P], in_=amp_a.rearrange("(s n) -> s n", s=4))
         load_x(1)
-        load_wb(0, 0)
-        load_x(2)
+        for q in range(4):
+            load_scale_rows(nc.sync, xs_raw[1], x_scales[:, :, W:NT], q)
         load_wb(1, 0)
+        load_x(2)
         load_x(3)
         load_wb(0, 1)
         load_wb(1, 1)
@@ -109,7 +116,7 @@ def tile_onebit_beam_crosscov_k4_kernel(
             )
             nc.vector.tensor_copy(
                 out=x_scl[s][:].bitcast(I32).rearrange("p g (t q r) -> p g t q r", t=4, r=2),
-                in_=xs_raw[:, :, P * s : P * (s + 1)].rearrange("p g (q t r) -> p g t q r", t=4, r=2),
+                in_=(xs_raw[1][:, :, P * (s - 1) : P * s] if s else xs_raw[0][:]).rearrange("p g (q t r) -> p g t q r", t=4, r=2),
             )
 
         def sort_rows():
@@ -132,19 +139,19 @@ def tile_onebit_beam_crosscov_k4_kernel(
                 in_=wb_raw[g, h][:, :, c0:c1].rearrange("p t (c i) -> p c t i", i=4),
             )
 
-        def quant_wb(g, h):
+        def quant_wb(g, h, c0, c1):
             nc.vector.quantize_mx(
-                out=wb_cod[g, h][:].bitcast(FP8X4),
-                scales=wb_scl[g, h][:],
-                in_=wb_grp[g, h][:].rearrange("p c t -> p (c t)"),
+                out=wb_cod[g, h][:, c0:c1].bitcast(FP8X4),
+                scales=wb_scl[g, h][:, c0:c1],
+                in_=wb_grp[g, h][:, c0:c1, :].rearrange("p c t -> p (c t)"),
             )
 
         hard = {}
 
         def beam_bank(i, b):
-            s = i % 4
             bank = ps_beam.tile([P, W], F32, name="beam", tag="beam")
             if i < 4:
+                s = i
                 j = b if i % 2 else (b + 3) % 4
                 for t in range(4):
                     for g in range(2):
@@ -159,8 +166,9 @@ def tile_onebit_beam_crosscov_k4_kernel(
                         )
                 slot, k = j, 4
             else:
-                h = i // 4 - 1
-                c = b // 2 if i % 2 else 1 - b // 2
+                h, c = divmod((i - 4) // 2, 2)
+                v = b // 2 if i % 2 else 1 - b // 2
+                s = 2 * (i % 2) + v
                 u = b % 2
                 for e in range(2):
                     t = 2 * u + e
@@ -174,7 +182,7 @@ def tile_onebit_beam_crosscov_k4_kernel(
                             start=(g == 0),
                             stop=(g == 1),
                         )
-                slot, k = 2 * c + u, 2
+                slot, k = 2 * v + u, 2
             nc.scalar.activation(
                 out=hard[i][:, W * slot : W * (slot + 1)].rearrange("p (n t) -> p n t", t=k),
                 in_=bank[:].rearrange("p (t n) -> p n t", t=k),
@@ -182,7 +190,6 @@ def tile_onebit_beam_crosscov_k4_kernel(
             )
 
         def weigh(engine, fac, i, w0, w1):
-            row = i % 4 if i < 4 else 4 + i % 4
             base = (W - GP_WORDS) * (i % 2)
             n = w1 - w0
             dst = u_ring[:, 4 * (base + w0) : 4 * (base + w1)]
@@ -190,44 +197,52 @@ def tile_onebit_beam_crosscov_k4_kernel(
                 engine.tensor_tensor(
                     out=dst.rearrange("p (n t) -> p n t", t=4),
                     in0=hard[i][:, 4 * w0 : 4 * w1].rearrange("p (n t) -> p n t", t=4),
-                    in1=fac[:, row : row + 1, :].to_broadcast([P, n, 4]),
+                    in1=fac[:, i : i + 1, :].to_broadcast([P, n, 4]),
                     op=MULT,
                 )
             else:
-                c = w0 // 256
+                v = w0 // 256
+                row = 4 + 2 * (i % 2) + v
                 engine.tensor_tensor(
                     out=dst.rearrange("p (n u e) -> p n u e", u=2, e=2),
-                    in0=hard[i][:].rearrange("p (c u n e) -> p c n u e", c=2, u=2, e=2)[
-                        :, c, w0 - 256 * c : w1 - 256 * c, :, :
+                    in0=hard[i][:].rearrange("p (v u n e) -> p v n u e", v=2, u=2, e=2)[
+                        :, v, w0 - 256 * v : w1 - 256 * v, :, :
                     ],
                     in1=fac[:, row : row + 1, :].rearrange("p o (u e) -> p o u e", u=2).to_broadcast([P, n, 2, 2]),
                     op=MULT,
                 )
 
-        def quant_u(i):
+        def quant_u(i, w0=0, w1=W):
             base = (W - GP_WORDS) * (i % 2)
             nc.vector.quantize_mx(
-                out=u_cod[i][:].bitcast(FP8X4), scales=u_scl[i][:], in_=u_ring[:, 4 * base : 4 * (base + W)]
+                out=u_cod[i][:, w0:w1].bitcast(FP8X4),
+                scales=u_scl[i][:, w0:w1],
+                in_=u_ring[:, 4 * (base + w0) : 4 * (base + w1)],
             )
 
         gram = {}
 
-        def gram_pass(j, h, s, pool=None):
-            if s == 0:
-                if pool is None:
-                    gram[j, h] = ps_gram.tile([P, W], F32, name="gram", tag="gram")
-                else:
-                    gram[j, h] = ps_beam.tile([P, W], F32, name="beam", tag="beam")
-            i = 4 + 4 * h + s
+        def gram_open(j, h, pool, tag):
+            gram[j, h] = pool.tile([P, W], F32, name=tag, tag=tag)
+
+        def gram_pass(j, i, v):
+            h, c = divmod((i - 4) // 2, 2)
+            s = 2 * (i % 2) + v
             nc.tensor.matmul_mx(
-                out=gram[j, h][:],
+                out=gram[j, h][:, 256 * c : 256 * (c + 1)],
                 lhsT=u_cod[s][:, P * j : P * (j + 1)].bitcast(FP8X4),
                 lhsT_scale=u_scl[s][:, P * j : P * (j + 1)],
-                rhs=u_cod[i][:].bitcast(FP8X4),
-                rhs_scale=u_scl[i][:],
+                rhs=u_cod[i][:, 256 * v : 256 * (v + 1)].bitcast(FP8X4),
+                rhs_scale=u_scl[i][:, 256 * v : 256 * (v + 1)],
                 start=(s == 0),
                 stop=(s == 3),
             )
+
+        def gram_steps(js, steps):
+            for j in js:
+                for i in steps:
+                    gram_pass(j, i, 0)
+                    gram_pass(j, i, 1)
 
         sine = {}
         y_f32 = {}
@@ -251,18 +266,15 @@ def tile_onebit_beam_crosscov_k4_kernel(
             )
             nc.sync.dma_start(out=out_0[P * j : P * (j + 1), W * h : W * (h + 1)], in_=y_f32[j, h][:])
 
-        def round_unit(j, h):
+        def round_unit(j, h, engine_copy=nc.vector.tensor_copy):
             y_bf[j, h] = stage.tile([P, W], BF16, name="y_bf", tag="y_bf", bufs=4)
-            nc.vector.tensor_copy(
+            engine_copy(
                 out=y_bf[j, h][:].rearrange("a (u p e) -> a u p e", u=2, e=2),
                 in_=y_f32[j, h][:].rearrange("a (p u e) -> a u p e", u=2, e=2),
             )
 
-        def turn_units(js, h, tail=False):
-            if tail:
-                bank = ps_beam.tile([P, W], F32, name="beam", tag="beam")
-            else:
-                bank = ps_one.tile([P, W], F32, name="turn", tag="turn")
+        def turn_units(js, h):
+            bank = ps_beam.tile([P, W], F32, name="beam", tag="beam")
             y_ps[js, h] = bank
             for k, j in enumerate(js):
                 words = y_bf[j, h][:].bitcast(F32)
@@ -273,7 +285,7 @@ def tile_onebit_beam_crosscov_k4_kernel(
 
         def copy_units(js, h):
             n = len(js)
-            y_grp[js, h] = stage.tile([P, 2 * W], BF16, name="y_grp", tag="y_grp", bufs=3, align_bytes=64)
+            y_grp[js, h] = stage.tile([P, 2 * W], BF16, name="y_grp", tag="y_grp", bufs=5, align_bytes=64)
             nc.scalar.copy(
                 out=y_grp[js, h][:, 0 : W * n].bitcast(F32).rearrange("p (k a u) -> p k a u", k=n, u=2),
                 in_=y_ps[js, h][:, 0 : 256 * n].rearrange("p (k u a) -> p k a u", k=n, u=2),
@@ -296,33 +308,44 @@ def tile_onebit_beam_crosscov_k4_kernel(
             )
 
         sort_x(0)
+        group_wb(nc.scalar.copy, 0, 0, 0, 256)
+        group_wb(nc.vector.tensor_copy, 0, 0, 256, W)
         for i in range(12):
             hard[i] = stage.tile([P, 4 * W], F32, name="hard", tag="hard", bufs=3)
             for b in range(4):
                 beam_bank(i, b)
-                if i == 0 and b == 0:
-                    sort_x(1)
-                if i == 0 and b == 3:
+                if i == 0 and b == 1:
                     sort_rows()
                     turn_rows()
+                    quant_wb(0, 0, 0, W)
                     nc.vector.tensor_copy(out=fac_sb[:], in_=fac_ps[:, 0 : AMP_ROW + 4, :])
-                if i == 10 and b < 2:
-                    sin_unit(b, 0)
-                if i == 11 and b < 2:
-                    sin_unit(2 + b, 0)
-            if 6 <= i <= 9:
-                gram_pass(0, 0, i - 6)
-                gram_pass(1, 0, i - 6)
+                    sort_x(1)
+                if i == 9 and b == 1:
+                    gram_steps(range(3), [7])
+                if i == 9 and b >= 2:
+                    sin_unit(b - 2, 0)
+                if i == 10 and b == 0:
+                    sin_unit(2, 0)
+                if i == 10 and b == 1:
+                    gram_open(3, 0, ps_gram, "gram")
+                    gram_steps([3], range(4, 8))
+                if i == 10 and b == 3:
+                    sin_unit(3, 0)
+            if i == 6:
+                for j in range(3):
+                    gram_open(j, 0, ps_gram, "gram")
+            if 6 <= i <= 8:
+                gram_steps(range(3), [i - 2])
             if i == 10:
-                for j in (2, 3):
-                    for s in range(4):
-                        gram_pass(j, 0, s)
-            if i == 0:
-                group_wb(nc.scalar.copy, 0, 0, 0, W)
-            if i in (1, 2):
-                group_wb(nc.scalar.copy, 1, 0, 256 * (i - 1), 256 * i)
+                gram_open(0, 1, ps_gram, "gram")
+                gram_open(1, 1, ps_gram, "gram")
+                gram_steps([0, 1], [8])
+            if i == 2:
+                group_wb(nc.scalar.copy, 1, 0, 256, W)
             if i in (4, 5):
-                group_wb(nc.scalar.copy, 0, 1, 256 * (i - 4), 256 * (i - 3))
+                group_wb(nc.scalar.copy, i - 4, 1, 0, 256)
+            if i == 7:
+                group_wb(nc.scalar.copy, 0, 1, 256, W)
             if i % 2:
                 gp, first, rest = (0, 128), (128, 256), [(256, 512)]
             else:
@@ -332,74 +355,80 @@ def tile_onebit_beam_crosscov_k4_kernel(
                     rest = [(256, 384), (384, 512)]
                 else:
                     first, rest = (0, 128), [(128, 256), (256, 384)]
-            if i == 0:
-                weigh(nc.vector, fac_ps, i, *gp)
+            weigh(nc.gpsimd, fac_sb, i, *gp)
             weigh(nc.vector, fac_ps, i, *first)
-            if i == 1:
-                sort_x(3)
-                quant_wb(0, 0)
-            if i == 3:
-                quant_wb(1, 0)
-            if i in (4, 5):
-                group_wb(nc.vector.tensor_copy, 1, 1, 256 * (i - 4), 256 * (i - 3))
-            if i == 6:
-                quant_wb(0, 1)
-                quant_wb(1, 1)
-            if i == 10:
-                scale_unit(0, 0)
-                scale_unit(1, 0)
-                round_unit(0, 0)
-            if i == 11:
-                round_unit(1, 0)
-                scale_unit(2, 0)
-                turn_units((0, 1), 0)
-                copy_units((0, 1), 0)
-            if i > 0:
-                quant_u(i - 1)
-                weigh(nc.gpsimd, fac_sb, i, *gp)
             for piece in rest:
                 weigh(nc.vector, fac_ps, i, *piece)
-            if i == 0:
-                sort_x(2)
+            if i in (0, 1):
+                sort_x(i + 2)
+            if i == 1:
+                group_wb(nc.vector.tensor_copy, 1, 0, 0, 256)
+            if i in (2, 3):
+                quant_wb(1, 0, 256 * (i - 2), 256 * (i - 1))
+            if i in (5, 6):
+                quant_wb(i - 5, 1, 0, 256)
+            if i == 7:
+                group_wb(nc.vector.tensor_copy, 1, 1, 256, W)
+            if i == 8:
+                quant_wb(0, 1, 256, W)
+                quant_wb(1, 1, 256, W)
+            if i == 9:
+                scale_unit(0, 0)
+            if i == 10:
+                scale_unit(2, 0)
+                scale_unit(3, 0)
+            if i in (4, 11):
+                quant_u(i, 0, 256)
+                quant_u(i, 256, W)
+            else:
+                quant_u(i)
+            if i == 9:
+                round_unit(0, 0)
+                scale_unit(1, 0)
 
-        for s in range(3):
-            gram_pass(0, 1, s)
-            gram_pass(1, 1, s)
-        for s in range(3):
-            gram_pass(2, 1, s, pool="beam")
-            gram_pass(3, 1, s, pool="beam")
-        scale_unit(3, 0)
-        quant_u(11)
-        for j in range(4):
-            gram_pass(j, 1, 3)
-        round_unit(2, 0)
-        quant_units((0, 1), 0)
-        round_unit(3, 0)
-        sin_unit(0, 1)
-        sin_unit(1, 1)
+        gram_open(2, 1, ps_gram, "gram")
+        gram_open(3, 1, ps_beam, "beam")
+        gram_steps([2, 3], [8])
+        round_unit(1, 0, nc.scalar.copy)
+        round_unit(2, 0, nc.scalar.copy)
+        round_unit(3, 0, nc.scalar.copy)
+        gram_steps(range(4), [9])
+        turn_units((0, 1), 0)
+        copy_units((0, 1), 0)
+        gram_steps(range(4), [10])
         turn_units((2, 3), 0)
         copy_units((2, 3), 0)
+        gram_pass(0, 11, 0)
+        gram_pass(1, 11, 0)
+        gram_pass(0, 11, 1)
+        gram_pass(1, 11, 1)
+        gram_steps([2, 3], [11])
+        quant_units((0, 1), 0)
+        quant_units((2, 3), 0)
+        store_codes(0, 0, NA, nc.sync)
+        for q in range(4):
+            store_scales(0, q, nc.sync)
+        sin_unit(0, 1)
+        sin_unit(1, 1)
         scale_unit(0, 1)
         sin_unit(2, 1)
         scale_unit(1, 1)
         sin_unit(3, 1)
         round_unit(0, 1)
-        quant_units((2, 3), 0)
-        store_codes(0, 0, NA, nc.sync)
-        for q in range(4):
-            store_scales(0, q, nc.sync)
-        round_unit(1, 1)
-        turn_units((0, 1), 1, tail=True)
-        copy_units((0, 1), 1)
         scale_unit(2, 1)
+        round_unit(1, 1)
         scale_unit(3, 1)
         round_unit(2, 1)
+        turn_units((0, 1), 1)
+        copy_units((0, 1), 1)
         round_unit(3, 1)
-        turn_units((2, 3), 1, tail=True)
-        copy_units((2, 3), 1)
+        turn_units((2,), 1)
+        copy_units((2,), 1)
+        turn_units((3,), 1)
+        copy_units((3,), 1)
         quant_units((0, 1), 1)
-        store_codes(1, 0, 256, nc.sync)
-        quant_units((2, 3), 1)
-        store_codes(1, 256, NA, nc.sync)
+        quant_units((2,), 1)
+        quant_units((3,), 1)
+        store_codes(1, 0, NA, nc.sync)
         for q in range(4):
             store_scales(1, q, nc.sync if q < 2 else nc.scalar)

@@ -18,7 +18,7 @@ MULT = mybir.AluOpType.mult
 
 P = 128
 W = 512
-GP_WORDS = 128
+GP_WORDS = 112
 AMP_ROW = 32
 
 
@@ -102,22 +102,29 @@ def tile_onebit_beam_crosscov_k4_kernel(
         load_x(1)
         for q in range(4):
             load_scale_rows(nc.sync, xs_raw[1], x_scales[:, :, W:NT], q)
-        load_wb(1, 0)
         load_x(2)
+        load_wb(1, 0)
         load_x(3)
         load_wb(0, 1)
         load_wb(1, 1)
         nc.sync.dma_start(out=amp_b_all[:], in_=amp_b.partition_broadcast(P))
 
-        def sort_x(s):
+        def sort_x_codes(s):
             nc.vector.tensor_copy(
                 out=x_cod[s][:].rearrange("p g (t q r) -> p g t q r", t=4, r=8),
                 in_=x_raw[s][:].rearrange("p g (q t r) -> p g t q r", t=4, r=8),
             )
+
+        def sort_x_scales(s):
+            raw = xs_raw[1][:, :, P * (s - 1) : P * s] if s else xs_raw[0][:]
             nc.vector.tensor_copy(
                 out=x_scl[s][:].bitcast(I32).rearrange("p g (t q r) -> p g t q r", t=4, r=2),
-                in_=(xs_raw[1][:, :, P * (s - 1) : P * s] if s else xs_raw[0][:]).rearrange("p g (q t r) -> p g t q r", t=4, r=2),
+                in_=raw.rearrange("p g (q t r) -> p g t q r", t=4, r=2),
             )
+
+        def sort_x(s):
+            sort_x_codes(s)
+            sort_x_scales(s)
 
         def sort_rows():
             nc.vector.tensor_copy(
@@ -152,7 +159,7 @@ def tile_onebit_beam_crosscov_k4_kernel(
             bank = ps_beam.tile([P, W], F32, name="beam", tag="beam")
             if i < 4:
                 s = i
-                j = b if i % 2 else (b + 3) % 4
+                j = b if i % 2 else 3 - b
                 for t in range(4):
                     for g in range(2):
                         nc.tensor.matmul_mx(
@@ -222,14 +229,18 @@ def tile_onebit_beam_crosscov_k4_kernel(
 
         gram = {}
 
-        def gram_open(j, h, pool, tag):
-            gram[j, h] = pool.tile([P, W], F32, name=tag, tag=tag)
+        def gram_open(js, h, cs, pool, tag):
+            bank = pool.tile([P, W], F32, name=tag, tag=tag)
+            parts = [(j, c) for j in js for c in cs]
+            for k, (j, c) in enumerate(parts):
+                gram[j, h, c] = bank[:, 256 * k : 256 * (k + 1)]
+            gram[js, h, cs] = bank[:, 0 : 256 * len(parts)]
 
         def gram_pass(j, i, v):
             h, c = divmod((i - 4) // 2, 2)
             s = 2 * (i % 2) + v
             nc.tensor.matmul_mx(
-                out=gram[j, h][:, 256 * c : 256 * (c + 1)],
+                out=gram[j, h, c],
                 lhsT=u_cod[s][:, P * j : P * (j + 1)].bitcast(FP8X4),
                 lhsT_scale=u_scl[s][:, P * j : P * (j + 1)],
                 rhs=u_cod[i][:, 256 * v : 256 * (v + 1)].bitcast(FP8X4),
@@ -250,27 +261,37 @@ def tile_onebit_beam_crosscov_k4_kernel(
         y_ps = {}
         y_grp = {}
 
-        def sin_unit(j, h):
-            sine[j, h] = stage.tile([P, W], F32, name="sine", tag="sine", bufs=3)
-            nc.scalar.activation(out=sine[j, h][:], in_=gram[j, h][:], func=ACT.Sin, scale=math.pi / 2)
+        def sin_bank(js, h, cs):
+            parts = [(j, c) for j in js for c in cs]
+            tile = stage.tile([P, W], F32, name="sine", tag="sine", bufs=4)
+            nc.scalar.activation(
+                out=tile[:, 0 : 256 * len(parts)], in_=gram[js, h, cs], func=ACT.Sin, scale=math.pi / 2
+            )
+            for k, j in enumerate(js):
+                sine[j, h, cs] = tile[:, 256 * len(cs) * k : 256 * len(cs) * (k + 1)]
 
-        def scale_unit(j, h):
-            y_f32[j, h] = stage.tile([P, W], F32, name="y_f32", tag="y_f32", bufs=4)
+        def scale_unit(j, h, cs=(0, 1)):
+            if cs[0] == 0:
+                y_f32[j, h] = stage.tile([P, W], F32, name="y_f32", tag="y_f32", bufs=6)
+            c0, c1 = 256 * cs[0], 256 * (cs[-1] + 1)
             nc.vector.scalar_tensor_tensor(
-                out=y_f32[j, h][:],
-                in0=sine[j, h][:],
+                out=y_f32[j, h][:, c0:c1],
+                in0=sine[j, h, cs],
                 scalar=fac_sb[:, AMP_ROW + j, 0:1],
-                in1=amp_b_all[:, W * h : W * (h + 1)],
+                in1=amp_b_all[:, W * h + c0 : W * h + c1],
                 op0=MULT,
                 op1=MULT,
             )
-            nc.sync.dma_start(out=out_0[P * j : P * (j + 1), W * h : W * (h + 1)], in_=y_f32[j, h][:])
+            if cs[-1] == 1:
+                nc.sync.dma_start(out=out_0[P * j : P * (j + 1), W * h : W * (h + 1)], in_=y_f32[j, h][:])
 
-        def round_unit(j, h, engine_copy=nc.vector.tensor_copy):
-            y_bf[j, h] = stage.tile([P, W], BF16, name="y_bf", tag="y_bf", bufs=4)
+        def round_unit(j, h, engine_copy=nc.vector.tensor_copy, cs=(0, 1)):
+            if cs[0] == 0:
+                y_bf[j, h] = stage.tile([P, W], BF16, name="y_bf", tag="y_bf", bufs=8)
+            p0, p1 = 64 * cs[0], 64 * (cs[-1] + 1)
             engine_copy(
-                out=y_bf[j, h][:].rearrange("a (u p e) -> a u p e", u=2, e=2),
-                in_=y_f32[j, h][:].rearrange("a (p u e) -> a u p e", u=2, e=2),
+                out=y_bf[j, h][:].rearrange("a (u p e) -> a u p e", u=2, e=2)[:, :, p0:p1, :],
+                in_=y_f32[j, h][:].rearrange("a (p u e) -> a u p e", u=2, e=2)[:, :, p0:p1, :],
             )
 
         def turn_units(js, h):
@@ -307,9 +328,10 @@ def tile_onebit_beam_crosscov_k4_kernel(
                 out=out_2[h, 4 * q : 4 * q + 4, :].bitcast(I32), in_=y_scl[h][32 * q : 32 * q + 4, :].bitcast(I32)
             )
 
+        both = (0, 1)
         sort_x(0)
-        group_wb(nc.scalar.copy, 0, 0, 0, 256)
-        group_wb(nc.vector.tensor_copy, 0, 0, 256, W)
+        group_wb(nc.scalar.copy, 0, 0, 0, 192)
+        group_wb(nc.vector.tensor_copy, 0, 0, 192, W)
         for i in range(12):
             hard[i] = stage.tile([P, 4 * W], F32, name="hard", tag="hard", bufs=3)
             for b in range(4):
@@ -318,66 +340,60 @@ def tile_onebit_beam_crosscov_k4_kernel(
                     sort_rows()
                     turn_rows()
                     quant_wb(0, 0, 0, W)
-                    nc.vector.tensor_copy(out=fac_sb[:], in_=fac_ps[:, 0 : AMP_ROW + 4, :])
                     sort_x(1)
+                    nc.vector.tensor_copy(out=fac_sb[:], in_=fac_ps[:, 0 : AMP_ROW + 4, :])
+                    sort_x(2)
                 if i == 9 and b == 1:
-                    gram_steps(range(3), [7])
+                    gram_steps(range(2), [7])
                 if i == 9 and b >= 2:
-                    sin_unit(b - 2, 0)
+                    sin_bank((b - 2,), 0, both)
                 if i == 10 and b == 0:
-                    sin_unit(2, 0)
+                    gram_steps([2], [6, 7])
                 if i == 10 and b == 1:
-                    gram_open(3, 0, ps_gram, "gram")
+                    sin_bank((2,), 0, both)
+                    gram_open((3,), 0, both, ps_gram, "gram")
                     gram_steps([3], range(4, 8))
                 if i == 10 and b == 3:
-                    sin_unit(3, 0)
+                    sin_bank((3,), 0, both)
+                if i == 11 and b == 1:
+                    gram_open((0, 1), 1, (0,), ps_gram, "gram")
+                    gram_steps([0, 1], [8, 9])
             if i == 6:
                 for j in range(3):
-                    gram_open(j, 0, ps_gram, "gram")
+                    gram_open((j,), 0, both, ps_gram, "gram")
             if 6 <= i <= 8:
-                gram_steps(range(3), [i - 2])
-            if i == 10:
-                gram_open(0, 1, ps_gram, "gram")
-                gram_open(1, 1, ps_gram, "gram")
-                gram_steps([0, 1], [8])
-            if i == 2:
-                group_wb(nc.scalar.copy, 1, 0, 256, W)
-            if i in (4, 5):
-                group_wb(nc.scalar.copy, i - 4, 1, 0, 256)
-            if i == 7:
+                gram_steps(range(3 if i < 8 else 2), [i - 2])
+            if i == 0:
+                group_wb(nc.scalar.copy, 1, 0, 0, 256)
+            if i in (3, 4):
+                group_wb(nc.scalar.copy, i - 3, 1, 0, 256)
+            if i == 6:
                 group_wb(nc.scalar.copy, 0, 1, 256, W)
             if i % 2:
-                gp, first, rest = (0, 128), (128, 256), [(256, 512)]
+                gp, first, rest = (0, GP_WORDS), (GP_WORDS, 256), (256, W)
             else:
-                gp, first, rest = (384, 512), (256, 384), [(0, 256)]
-            if i < 4:
-                if i % 2:
-                    rest = [(256, 384), (384, 512)]
-                else:
-                    first, rest = (0, 128), [(128, 256), (256, 384)]
+                gp, first, rest = (W - GP_WORDS, W), (256, W - GP_WORDS), (0, 256)
             weigh(nc.gpsimd, fac_sb, i, *gp)
             weigh(nc.vector, fac_ps, i, *first)
-            for piece in rest:
-                weigh(nc.vector, fac_ps, i, *piece)
-            if i in (0, 1):
-                sort_x(i + 2)
+            weigh(nc.vector, fac_ps, i, *rest)
+            if i == 0:
+                sort_x(3)
             if i == 1:
-                group_wb(nc.vector.tensor_copy, 1, 0, 0, 256)
+                group_wb(nc.vector.tensor_copy, 1, 0, 256, W)
             if i in (2, 3):
                 quant_wb(1, 0, 256 * (i - 2), 256 * (i - 1))
-            if i in (5, 6):
-                quant_wb(i - 5, 1, 0, 256)
-            if i == 7:
+            if i in (4, 5):
+                quant_wb(i - 4, 1, 0, 256)
+            if i == 6:
                 group_wb(nc.vector.tensor_copy, 1, 1, 256, W)
-            if i == 8:
-                quant_wb(0, 1, 256, W)
-                quant_wb(1, 1, 256, W)
+            if i in (7, 8):
+                quant_wb(8 - i, 1, 256, W)
             if i == 9:
                 scale_unit(0, 0)
             if i == 10:
                 scale_unit(2, 0)
                 scale_unit(3, 0)
-            if i in (4, 11):
+            if i == 11:
                 quant_u(i, 0, 256)
                 quant_u(i, 256, W)
             else:
@@ -386,16 +402,21 @@ def tile_onebit_beam_crosscov_k4_kernel(
                 round_unit(0, 0)
                 scale_unit(1, 0)
 
-        gram_open(2, 1, ps_gram, "gram")
-        gram_open(3, 1, ps_beam, "beam")
-        gram_steps([2, 3], [8])
+        gram_open((2, 3), 1, (0,), ps_gram, "gram")
+        gram_steps([2, 3], [8, 9])
         round_unit(1, 0, nc.scalar.copy)
+        sin_bank((0, 1), 1, (0,))
         round_unit(2, 0, nc.scalar.copy)
         round_unit(3, 0, nc.scalar.copy)
-        gram_steps(range(4), [9])
+        sin_bank((2, 3), 1, (0,))
+        gram_open((0,), 1, (1,), ps_gram, "gram")
+        gram_open((1,), 1, (1,), ps_beam, "beam")
+        gram_open((2,), 1, (1,), ps_beam, "beam")
+        gram_steps([0, 1, 2], [10])
         turn_units((0, 1), 0)
         copy_units((0, 1), 0)
-        gram_steps(range(4), [10])
+        gram_open((3,), 1, (1,), ps_gram, "gram")
+        gram_steps([3], [10])
         turn_units((2, 3), 0)
         copy_units((2, 3), 0)
         gram_pass(0, 11, 0)
@@ -403,25 +424,29 @@ def tile_onebit_beam_crosscov_k4_kernel(
         gram_pass(0, 11, 1)
         gram_pass(1, 11, 1)
         gram_steps([2, 3], [11])
+        for j in range(4):
+            scale_unit(j, 1, (0,))
         quant_units((0, 1), 0)
         quant_units((2, 3), 0)
         store_codes(0, 0, NA, nc.sync)
         for q in range(4):
             store_scales(0, q, nc.sync)
-        sin_unit(0, 1)
-        sin_unit(1, 1)
-        scale_unit(0, 1)
-        sin_unit(2, 1)
-        scale_unit(1, 1)
-        sin_unit(3, 1)
-        round_unit(0, 1)
-        scale_unit(2, 1)
-        round_unit(1, 1)
-        scale_unit(3, 1)
-        round_unit(2, 1)
+        for j in range(4):
+            sin_bank((j,), 1, (1,))
+        round_unit(0, 1, cs=(0,))
+        scale_unit(0, 1, (1,))
+        round_unit(1, 1, cs=(0,))
+        scale_unit(1, 1, (1,))
+        round_unit(0, 1, cs=(1,))
+        scale_unit(2, 1, (1,))
+        round_unit(1, 1, cs=(1,))
         turn_units((0, 1), 1)
+        round_unit(2, 1, nc.scalar.copy, cs=(0,))
+        round_unit(3, 1, nc.scalar.copy, cs=(0,))
         copy_units((0, 1), 1)
-        round_unit(3, 1)
+        scale_unit(3, 1, (1,))
+        round_unit(2, 1, cs=(1,))
+        round_unit(3, 1, cs=(1,))
         turn_units((2,), 1)
         copy_units((2,), 1)
         turn_units((3,), 1)

@@ -18,7 +18,7 @@ MULT = mybir.AluOpType.mult
 
 P = 128
 W = 512
-GP_WORDS = 112
+GP_WORDS = 128
 AMP_ROW = 32
 
 
@@ -57,15 +57,14 @@ def tile_onebit_beam_crosscov_k4_kernel(
         fac_sb = kept("fac_sb", [P, AMP_ROW + 4, 4], F32)
         amp_b_all = kept("amp_b_all", [P, NB], BF16)
         y_cod = [kept("y_cod%d" % h, [P, NA], I32) for h in range(2)]
-        y_scl = [kept("y_scl%d" % h, [P, NA], U8) for h in range(2)]
+        y_scl = kept("y_scl", [P, 2, NA], U8)
         fac_ps = ps_one.tile([P, P, 4], F32, name="fac_ps")
 
-        nc.vector.memset(wa_scl[:].bitcast(I32), 0)
+        nc.gpsimd.memset(wa_scl[:].bitcast(I32), 0)
+        nc.gpsimd.memset(xs_raw[0][:], 0)
         nc.vector.memset(warm[:, 0:1], 0.0)
-        nc.vector.memset(xs_raw[0][:], 0)
         nc.vector.memset(xs_raw[1][:], 0)
         nc.vector.memset(rows_f32[:], 0.0)
-        nc.scalar.activation(out=warm[:, 1:2], in_=warm[:, 0:1], func=ACT.Silu)
 
         x_view = x_words.rearrange("g p n t -> p g (n t)")
 
@@ -85,17 +84,17 @@ def tile_onebit_beam_crosscov_k4_kernel(
             )
 
         wa_scl_words = wa_scl[:].bitcast(I32)
-        for q in range(3):
+        nc.scalar.activation(out=warm[:, 1:2], in_=warm[:, 0:1], func=ACT.Silu)
+        for q in range(2):
             load_scale_rows(nc.sync, wa_scl_words, wa_scales, q)
         load_x(0)
         nc.sync.dma_start(out=wa_cod[:].bitcast(I32), in_=wa_words.rearrange("g p n -> p g n").bitcast(I32))
-        load_scale_rows(nc.sync, xs_raw[0], x_scales[:, :, 0:W], 0)
-        load_scale_rows(nc.sync, xs_raw[0], x_scales[:, :, 0:W], 2)
-        load_wb(0, 0)
-        load_scale_rows(nc.sync, xs_raw[0], x_scales[:, :, 0:W], 1)
-        load_scale_rows(nc.sync, xs_raw[0], x_scales[:, :, 0:W], 3)
-        load_scale_rows(nc.sync, wa_scl_words, wa_scales, 3)
+        for q in range(4):
+            load_scale_rows(nc.sync, xs_raw[0], x_scales[:, :, 0:W], q)
+        for q in range(2, 4):
+            load_scale_rows(nc.sync, wa_scl_words, wa_scales, q)
         make_identity(nc, ident[:])
+        load_wb(0, 0)
         nc.sync.dma_start(out=rows_raw[0:4, :], in_=snap_a.rearrange("(s n) -> s n", s=4))
         nc.sync.dma_start(out=rows_raw[4:8, :], in_=snap_b.rearrange("(s n) -> s n", s=4))
         nc.sync.dma_start(out=rows_raw[AMP_ROW : AMP_ROW + 4, 0:P], in_=amp_a.rearrange("(s n) -> s n", s=4))
@@ -306,7 +305,7 @@ def tile_onebit_beam_crosscov_k4_kernel(
 
         def copy_units(js, h):
             n = len(js)
-            y_grp[js, h] = stage.tile([P, 2 * W], BF16, name="y_grp", tag="y_grp", bufs=5, align_bytes=64)
+            y_grp[js, h] = stage.tile([P, 2 * W], BF16, name="y_grp", tag="y_grp", bufs=6, align_bytes=64)
             nc.scalar.copy(
                 out=y_grp[js, h][:, 0 : W * n].bitcast(F32).rearrange("p (k a u) -> p k a u", k=n, u=2),
                 in_=y_ps[js, h][:, 0 : 256 * n].rearrange("p (k u a) -> p k a u", k=n, u=2),
@@ -315,7 +314,7 @@ def tile_onebit_beam_crosscov_k4_kernel(
         def quant_units(js, h):
             cols = slice(P * js[0], P * (js[-1] + 1))
             nc.vector.quantize_mx(
-                out=y_cod[h][:, cols].bitcast(FP8X4), scales=y_scl[h][:, cols], in_=y_grp[js, h][:, 0 : W * len(js)]
+                out=y_cod[h][:, cols].bitcast(FP8X4), scales=y_scl[:, h, cols], in_=y_grp[js, h][:, 0 : W * len(js)]
             )
 
         def store_codes(h, c0, c1, queue):
@@ -323,26 +322,27 @@ def tile_onebit_beam_crosscov_k4_kernel(
                 out=out_1[h].rearrange("p m t -> p (m t)")[:, 4 * c0 : 4 * c1].bitcast(I32), in_=y_cod[h][:, c0:c1]
             )
 
-        def store_scales(h, q, queue):
+        def store_scales(q, queue):
             queue.dma_start(
-                out=out_2[h, 4 * q : 4 * q + 4, :].bitcast(I32), in_=y_scl[h][32 * q : 32 * q + 4, :].bitcast(I32)
+                out=out_2[:, 4 * q : 4 * q + 4, :].rearrange("g r m -> r g m").bitcast(I32),
+                in_=y_scl[32 * q : 32 * q + 4, :, :].bitcast(I32),
             )
 
         both = (0, 1)
         sort_x(0)
-        group_wb(nc.scalar.copy, 0, 0, 0, 192)
-        group_wb(nc.vector.tensor_copy, 0, 0, 192, W)
         for i in range(12):
             hard[i] = stage.tile([P, 4 * W], F32, name="hard", tag="hard", bufs=3)
             for b in range(4):
                 beam_bank(i, b)
                 if i == 0 and b == 1:
+                    group_wb(nc.vector.tensor_copy, 0, 0, 0, 256)
                     sort_rows()
                     turn_rows()
+                    group_wb(nc.vector.tensor_copy, 0, 0, 256, W)
+                    sort_x_codes(1)
                     quant_wb(0, 0, 0, W)
-                    sort_x(1)
+                    sort_x_scales(1)
                     nc.vector.tensor_copy(out=fac_sb[:], in_=fac_ps[:, 0 : AMP_ROW + 4, :])
-                    sort_x(2)
                 if i == 9 and b == 1:
                     gram_steps(range(2), [7])
                 if i == 9 and b >= 2:
@@ -363,11 +363,11 @@ def tile_onebit_beam_crosscov_k4_kernel(
                     gram_open((j,), 0, both, ps_gram, "gram")
             if 6 <= i <= 8:
                 gram_steps(range(3 if i < 8 else 2), [i - 2])
-            if i == 0:
+            if i == 1:
                 group_wb(nc.scalar.copy, 1, 0, 0, 256)
-            if i in (3, 4):
-                group_wb(nc.scalar.copy, i - 3, 1, 0, 256)
-            if i == 6:
+            if i == 3:
+                group_wb(nc.scalar.copy, 1, 0, 256, W)
+            if i == 7:
                 group_wb(nc.scalar.copy, 0, 1, 256, W)
             if i % 2:
                 gp, first, rest = (0, GP_WORDS), (GP_WORDS, 256), (256, W)
@@ -376,31 +376,32 @@ def tile_onebit_beam_crosscov_k4_kernel(
             weigh(nc.gpsimd, fac_sb, i, *gp)
             weigh(nc.vector, fac_ps, i, *first)
             weigh(nc.vector, fac_ps, i, *rest)
-            if i == 0:
-                sort_x(3)
-            if i == 1:
-                group_wb(nc.vector.tensor_copy, 1, 0, 256, W)
-            if i in (2, 3):
-                quant_wb(1, 0, 256 * (i - 2), 256 * (i - 1))
-            if i in (4, 5):
-                quant_wb(i - 4, 1, 0, 256)
+            if i in (0, 1):
+                sort_x(i + 2)
+            if i in (2, 4):
+                quant_wb(1, 0, 128 * (i - 2), 128 * i)
+            if i in (3, 7):
+                group_wb(nc.vector.tensor_copy, 1, 1, 64 * (i - 3), 64 * (i + 1))
+            if i == 5:
+                quant_wb(1, 1, 0, 256)
+                group_wb(nc.vector.tensor_copy, 0, 1, 0, 256)
             if i == 6:
-                group_wb(nc.vector.tensor_copy, 1, 1, 256, W)
-            if i in (7, 8):
-                quant_wb(8 - i, 1, 256, W)
+                quant_wb(0, 1, 0, 256)
+            if i == 8:
+                quant_wb(0, 1, 256, W)
+                quant_wb(1, 1, 256, W)
             if i == 9:
                 scale_unit(0, 0)
+                scale_unit(1, 0)
             if i == 10:
                 scale_unit(2, 0)
+                round_unit(0, 0)
                 scale_unit(3, 0)
             if i == 11:
                 quant_u(i, 0, 256)
                 quant_u(i, 256, W)
             else:
                 quant_u(i)
-            if i == 9:
-                round_unit(0, 0)
-                scale_unit(1, 0)
 
         gram_open((2, 3), 1, (0,), ps_gram, "gram")
         gram_steps([2, 3], [8, 9])
@@ -417,43 +418,39 @@ def tile_onebit_beam_crosscov_k4_kernel(
         copy_units((0, 1), 0)
         gram_open((3,), 1, (1,), ps_gram, "gram")
         gram_steps([3], [10])
-        turn_units((2, 3), 0)
-        copy_units((2, 3), 0)
         gram_pass(0, 11, 0)
         gram_pass(1, 11, 0)
         gram_pass(0, 11, 1)
         gram_pass(1, 11, 1)
         gram_steps([2, 3], [11])
+        turn_units((2, 3), 0)
         for j in range(4):
             scale_unit(j, 1, (0,))
-        quant_units((0, 1), 0)
-        quant_units((2, 3), 0)
-        store_codes(0, 0, NA, nc.sync)
-        for q in range(4):
-            store_scales(0, q, nc.sync)
+        round_unit(0, 1, cs=(0,))
+        round_unit(1, 1, cs=(0,))
         for j in range(4):
             sin_bank((j,), 1, (1,))
-        round_unit(0, 1, cs=(0,))
+        quant_units((0, 1), 0)
         scale_unit(0, 1, (1,))
-        round_unit(1, 1, cs=(0,))
         scale_unit(1, 1, (1,))
         round_unit(0, 1, cs=(1,))
         scale_unit(2, 1, (1,))
         round_unit(1, 1, cs=(1,))
-        turn_units((0, 1), 1)
         round_unit(2, 1, nc.scalar.copy, cs=(0,))
         round_unit(3, 1, nc.scalar.copy, cs=(0,))
-        copy_units((0, 1), 1)
+        copy_units((2, 3), 0)
         scale_unit(3, 1, (1,))
         round_unit(2, 1, cs=(1,))
         round_unit(3, 1, cs=(1,))
-        turn_units((2,), 1)
-        copy_units((2,), 1)
-        turn_units((3,), 1)
-        copy_units((3,), 1)
-        quant_units((0, 1), 1)
-        quant_units((2,), 1)
-        quant_units((3,), 1)
-        store_codes(1, 0, NA, nc.sync)
+        quant_units((2, 3), 0)
+        store_codes(0, 0, NA, nc.sync)
+        for j in range(4):
+            turn_units((j,), 1)
+            copy_units((j,), 1)
+        for j in range(4):
+            quant_units((j,), 1)
+            if j == 2:
+                store_codes(1, 0, 3 * P, nc.sync)
+        store_codes(1, 3 * P, NA, nc.scalar)
         for q in range(4):
-            store_scales(1, q, nc.sync if q < 2 else nc.scalar)
+            store_scales(q, nc.sync if q < 2 else nc.scalar)

import math
from contextlib import ExitStack

import concourse.mybir as mybir
from concourse.masks import make_identity

NS, NT, NA, NB = 1024, 2048, 512, 1024
FLOPS = 2 * NT * NS * (NA + NB) + 2 * NT * NA * NB

F32 = mybir.dt.float32
BF16 = mybir.dt.bfloat16
I32 = mybir.dt.int32
U8 = mybir.dt.uint8
FP8X4 = mybir.dt.float8_e4m3fn_x4
FP4X4 = mybir.dt.float4_e2m1fn_x4
ACT = mybir.ActivationFunctionType
MULT = mybir.AluOpType.mult

P = 128
W = 512
GP_WORDS = 128
AMP_ROW = 32


def tile_onebit_beam_crosscov_k4_kernel(
    tc, x_words, x_scales, wa_words, wa_scales, wb, snap_a, snap_b, amp_a, amp_b, out_0, out_1, out_2
):
    nc = tc.nc
    with ExitStack() as ctx:
        keep = ctx.enter_context(tc.tile_pool(name="keep", bufs=1))
        stage = ctx.enter_context(tc.tile_pool(name="stage", bufs=2))
        ps_one = ctx.enter_context(tc.psum_pool(name="ps_one", bufs=1))
        ps_gram = ctx.enter_context(tc.psum_pool(name="ps_gram", bufs=3))
        ps_beam = ctx.enter_context(tc.psum_pool(name="ps_beam", bufs=4))
        ctx.enter_context(tc.manual_schedule())

        def kept(name, shape, dtype):
            return keep.tile(shape, dtype, name=name, align_bytes=64)

        x_raw = [kept("x_raw%d" % s, [P, 2, W], I32) for s in range(4)]
        x_cod = [kept("x_cod%d" % s, [P, 2, W], I32) for s in range(4)]
        xs_raw = [kept("xs_raw0", [P, 2, P], I32), kept("xs_raw1", [P, 2, 3 * P], I32)]
        x_scl = [kept("x_scl%d" % s, [P, 2, W], U8) for s in range(4)]
        wa_cod = kept("wa_cod", [P, 2, 2 * NA], U8)
        wa_scl = kept("wa_scl", [P, 2, NA], U8)
        wb_raw = {(g, h): kept("wb_raw%d%d" % (g, h), [P, 4, W], BF16) for g in range(2) for h in range(2)}
        wb_grp = {(g, h): kept("wb_grp%d%d" % (g, h), [P, W, 4], BF16) for g in range(2) for h in range(2)}
        wb_cod = {(g, h): kept("wb_cod%d%d" % (g, h), [P, W], I32) for g in range(2) for h in range(2)}
        wb_scl = {(g, h): kept("wb_scl%d%d" % (g, h), [P, W], U8) for g in range(2) for h in range(2)}
        u_cod = [kept("u_cod%d" % i, [P, W], I32) for i in range(12)]
        u_scl = [kept("u_scl%d" % i, [P, W], U8) for i in range(12)]
        u_ring = kept("u_ring", [P, 4 * (2 * W - GP_WORDS)], BF16)
        rows_raw = kept("rows_raw", [P, W], BF16)
        rows_f32 = kept("rows_f32", [P, 4, P], F32)
        ident = kept("ident", [P, P], F32)
        warm = kept("warm", [P, 2], F32)
        fac_sb = kept("fac_sb", [P, AMP_ROW + 4, 4], F32)
        amp_b_all = kept("amp_b_all", [P, NB], BF16)
        y_cod = [kept("y_cod%d" % h, [P, NA], I32) for h in range(2)]
        y_scl = kept("y_scl", [P, 2, NA], U8)
        fac_ps = ps_one.tile([P, P, 4], F32, name="fac_ps")

        nc.gpsimd.memset(wa_scl[:].bitcast(I32), 0)
        nc.gpsimd.memset(xs_raw[0][:], 0)
        nc.vector.memset(warm[:, 0:1], 0.0)
        nc.vector.memset(xs_raw[1][:], 0)
        nc.vector.memset(rows_f32[:], 0.0)

        x_view = x_words.rearrange("g p n t -> p g (n t)")

        def load_x(s):
            nc.sync.dma_start(out=x_raw[s][:], in_=x_view[:, :, 4 * W * s : 4 * W * (s + 1)].bitcast(I32))

        def load_wb(g, h):
            nc.sync.dma_start(
                out=wb_raw[g, h][:],
                in_=wb[W * g : W * (g + 1), W * h : W * (h + 1)].rearrange("(p t) n -> p t n", t=4),
            )

        def load_scale_rows(queue, plane, scales, q):
            queue.dma_start(
                out=plane[32 * q : 32 * q + 4, :, :],
                in_=scales[:, 4 * q : 4 * q + 4, :].rearrange("g r n -> r g n").bitcast(I32),
            )

        wa_scl_words = wa_scl[:].bitcast(I32)
        nc.scalar.activation(out=warm[:, 1:2], in_=warm[:, 0:1], func=ACT.Silu)
        for q in range(2):
            load_scale_rows(nc.sync, wa_scl_words, wa_scales, q)
        load_x(0)
        nc.sync.dma_start(out=wa_cod[:].bitcast(I32), in_=wa_words.rearrange("g p n -> p g n").bitcast(I32))
        for q in range(4):
            load_scale_rows(nc.sync, xs_raw[0], x_scales[:, :, 0:W], q)
        for q in range(2, 4):
            load_scale_rows(nc.sync, wa_scl_words, wa_scales, q)
        make_identity(nc, ident[:])
        load_wb(0, 0)
        nc.sync.dma_start(out=rows_raw[0:4, :], in_=snap_a.rearrange("(s n) -> s n", s=4))
        nc.sync.dma_start(out=rows_raw[4:8, :], in_=snap_b.rearrange("(s n) -> s n", s=4))
        nc.sync.dma_start(out=rows_raw[AMP_ROW : AMP_ROW + 4, 0:P], in_=amp_a.rearrange("(s n) -> s n", s=4))
        load_x(1)
        for q in range(4):
            load_scale_rows(nc.sync, xs_raw[1], x_scales[:, :, W:NT], q)
        load_x(2)
        load_wb(1, 0)
        load_x(3)
        load_wb(0, 1)
        load_wb(1, 1)
        nc.sync.dma_start(out=amp_b_all[:], in_=amp_b.partition_broadcast(P))

        def sort_x_codes(s):
            nc.vector.tensor_copy(
                out=x_cod[s][:].rearrange("p g (t q r) -> p g t q r", t=4, r=8),
                in_=x_raw[s][:].rearrange("p g (q t r) -> p g t q r", t=4, r=8),
            )

        def sort_x_scales(s):
            raw = xs_raw[1][:, :, P * (s - 1) : P * s] if s else xs_raw[0][:]
            nc.vector.tensor_copy(
                out=x_scl[s][:].bitcast(I32).rearrange("p g (t q r) -> p g t q r", t=4, r=2),
                in_=raw.rearrange("p g (q t r) -> p g t q r", t=4, r=2),
            )

        def sort_x(s):
            sort_x_codes(s)
            sort_x_scales(s)

        def sort_rows():
            nc.vector.tensor_copy(
                out=rows_f32[0:8, :, :].rearrange("s t (q r) -> s t q r", r=8),
                in_=rows_raw[0:8, :].rearrange("s (q t r) -> s t q r", t=4, r=8),
            )
            nc.vector.tensor_copy(
                out=rows_f32[AMP_ROW : AMP_ROW + 4, 0, :],
                in_=rows_raw[AMP_ROW : AMP_ROW + 4, 0:P],
            )

        def turn_rows():
            for t in range(4):
                nc.tensor.transpose(fac_ps[:, :, t], rows_f32[:, t, :], ident[:])

        def group_wb(engine_copy, g, h, c0, c1):
            engine_copy(
                out=wb_grp[g, h][:, c0:c1, :].rearrange("p (c i) t -> p c t i", i=4),
                in_=wb_raw[g, h][:, :, c0:c1].rearrange("p t (c i) -> p c t i", i=4),
            )

        def quant_wb(g, h, c0, c1):
            nc.vector.quantize_mx(
                out=wb_cod[g, h][:, c0:c1].bitcast(FP8X4),
                scales=wb_scl[g, h][:, c0:c1],
                in_=wb_grp[g, h][:, c0:c1, :].rearrange("p c t -> p (c t)"),
            )

        hard = {}

        def beam_bank(i, b):
            bank = ps_beam.tile([P, W], F32, name="beam", tag="beam")
            if i < 4:
                s = i
                j = b if i % 2 else 3 - b
                for t in range(4):
                    for g in range(2):
                        nc.tensor.matmul_mx(
                            out=bank[:, P * t : P * (t + 1)],
                            lhsT=x_cod[s][:, g, P * t : P * (t + 1)].bitcast(FP8X4),
                            lhsT_scale=x_scl[s][:, g, P * t : P * (t + 1)],
                            rhs=wa_cod[:, g, 2 * P * j : 2 * P * (j + 1)].bitcast(FP4X4),
                            rhs_scale=wa_scl[:, g, P * j : P * (j + 1)],
                            start=(g == 0),
                            stop=(g == 1),
                        )
                slot, k = j, 4
            else:
                h, c = divmod((i - 4) // 2, 2)
                v = b // 2 if i % 2 else 1 - b // 2
                s = 2 * (i % 2) + v
                u = b % 2
                for e in range(2):
                    t = 2 * u + e
                    for g in range(2):
                        nc.tensor.matmul_mx(
                            out=bank[:, 256 * e : 256 * (e + 1)],
                            lhsT=x_cod[s][:, g, P * t : P * (t + 1)].bitcast(FP8X4),
                            lhsT_scale=x_scl[s][:, g, P * t : P * (t + 1)],
                            rhs=wb_cod[g, h][:, 256 * c : 256 * (c + 1)].bitcast(FP8X4),
                            rhs_scale=wb_scl[g, h][:, 256 * c : 256 * (c + 1)],
                            start=(g == 0),
                            stop=(g == 1),
                        )
                slot, k = 2 * v + u, 2
            nc.scalar.activation(
                out=hard[i][:, W * slot : W * (slot + 1)].rearrange("p (n t) -> p n t", t=k),
                in_=bank[:].rearrange("p (t n) -> p n t", t=k),
                func=ACT.Tanh,
            )

        def weigh(engine, fac, i, w0, w1):
            base = (W - GP_WORDS) * (i % 2)
            n = w1 - w0
            dst = u_ring[:, 4 * (base + w0) : 4 * (base + w1)]
            if i < 4:
                engine.tensor_tensor(
                    out=dst.rearrange("p (n t) -> p n t", t=4),
                    in0=hard[i][:, 4 * w0 : 4 * w1].rearrange("p (n t) -> p n t", t=4),
                    in1=fac[:, i : i + 1, :].to_broadcast([P, n, 4]),
                    op=MULT,
                )
            else:
                v = w0 // 256
                row = 4 + 2 * (i % 2) + v
                engine.tensor_tensor(
                    out=dst.rearrange("p (n u e) -> p n u e", u=2, e=2),
                    in0=hard[i][:].rearrange("p (v u n e) -> p v n u e", v=2, u=2, e=2)[
                        :, v, w0 - 256 * v : w1 - 256 * v, :, :
                    ],
                    in1=fac[:, row : row + 1, :].rearrange("p o (u e) -> p o u e", u=2).to_broadcast([P, n, 2, 2]),
                    op=MULT,
                )

        def quant_u(i, w0=0, w1=W):
            base = (W - GP_WORDS) * (i % 2)
            nc.vector.quantize_mx(
                out=u_cod[i][:, w0:w1].bitcast(FP8X4),
                scales=u_scl[i][:, w0:w1],
                in_=u_ring[:, 4 * (base + w0) : 4 * (base + w1)],
            )

        gram = {}

        def gram_open(js, h, cs, pool, tag):
            bank = pool.tile([P, W], F32, name=tag, tag=tag)
            parts = [(j, c) for j in js for c in cs]
            for k, (j, c) in enumerate(parts):
                gram[j, h, c] = bank[:, 256 * k : 256 * (k + 1)]
            gram[js, h, cs] = bank[:, 0 : 256 * len(parts)]

        def gram_pass(j, i, v):
            h, c = divmod((i - 4) // 2, 2)
            s = 2 * (i % 2) + v
            nc.tensor.matmul_mx(
                out=gram[j, h, c],
                lhsT=u_cod[s][:, P * j : P * (j + 1)].bitcast(FP8X4),
                lhsT_scale=u_scl[s][:, P * j : P * (j + 1)],
                rhs=u_cod[i][:, 256 * v : 256 * (v + 1)].bitcast(FP8X4),
                rhs_scale=u_scl[i][:, 256 * v : 256 * (v + 1)],
                start=(s == 0),
                stop=(s == 3),
            )

        def gram_steps(js, steps):
            for j in js:
                for i in steps:
                    gram_pass(j, i, 0)
                    gram_pass(j, i, 1)

        sine = {}
        y_f32 = {}
        y_bf = {}
        y_ps = {}
        y_grp = {}

        def sin_bank(js, h, cs):
            parts = [(j, c) for j in js for c in cs]
            tile = stage.tile([P, W], F32, name="sine", tag="sine", bufs=4)
            nc.scalar.activation(
                out=tile[:, 0 : 256 * len(parts)], in_=gram[js, h, cs], func=ACT.Sin, scale=math.pi / 2
            )
            for k, j in enumerate(js):
                sine[j, h, cs] = tile[:, 256 * len(cs) * k : 256 * len(cs) * (k + 1)]

        def scale_unit(j, h, cs=(0, 1)):
            if cs[0] == 0:
                y_f32[j, h] = stage.tile([P, W], F32, name="y_f32", tag="y_f32", bufs=6)
            c0, c1 = 256 * cs[0], 256 * (cs[-1] + 1)
            nc.vector.scalar_tensor_tensor(
                out=y_f32[j, h][:, c0:c1],
                in0=sine[j, h, cs],
                scalar=fac_sb[:, AMP_ROW + j, 0:1],
                in1=amp_b_all[:, W * h + c0 : W * h + c1],
                op0=MULT,
                op1=MULT,
            )
            if cs[-1] == 1:
                nc.sync.dma_start(out=out_0[P * j : P * (j + 1), W * h : W * (h + 1)], in_=y_f32[j, h][:])

        def round_unit(j, h, engine_copy=nc.vector.tensor_copy, cs=(0, 1)):
            if cs[0] == 0:
                y_bf[j, h] = stage.tile([P, W], BF16, name="y_bf", tag="y_bf", bufs=8)
            p0, p1 = 64 * cs[0], 64 * (cs[-1] + 1)
            engine_copy(
                out=y_bf[j, h][:].rearrange("a (u p e) -> a u p e", u=2, e=2)[:, :, p0:p1, :],
                in_=y_f32[j, h][:].rearrange("a (p u e) -> a u p e", u=2, e=2)[:, :, p0:p1, :],
            )

        def turn_units(js, h):
            bank = ps_beam.tile([P, W], F32, name="beam", tag="beam")
            y_ps[js, h] = bank
            for k, j in enumerate(js):
                words = y_bf[j, h][:].bitcast(F32)
                for u in range(2):
                    nc.tensor.transpose(
                        bank[:, 256 * k + P * u : 256 * k + P * (u + 1)], words[:, P * u : P * (u + 1)], ident[:]
                    )

        def copy_units(js, h):
            n = len(js)
            y_grp[js, h] = stage.tile([P, 2 * W], BF16, name="y_grp", tag="y_grp", bufs=6, align_bytes=64)
            nc.scalar.copy(
                out=y_grp[js, h][:, 0 : W * n].bitcast(F32).rearrange("p (k a u) -> p k a u", k=n, u=2),
                in_=y_ps[js, h][:, 0 : 256 * n].rearrange("p (k u a) -> p k a u", k=n, u=2),
            )

        def quant_units(js, h):
            cols = slice(P * js[0], P * (js[-1] + 1))
            nc.vector.quantize_mx(
                out=y_cod[h][:, cols].bitcast(FP8X4), scales=y_scl[:, h, cols], in_=y_grp[js, h][:, 0 : W * len(js)]
            )

        def store_codes(h, c0, c1, queue):
            queue.dma_start(
                out=out_1[h].rearrange("p m t -> p (m t)")[:, 4 * c0 : 4 * c1].bitcast(I32), in_=y_cod[h][:, c0:c1]
            )

        def store_scales(q, queue):
            queue.dma_start(
                out=out_2[:, 4 * q : 4 * q + 4, :].rearrange("g r m -> r g m").bitcast(I32),
                in_=y_scl[32 * q : 32 * q + 4, :, :].bitcast(I32),
            )

        both = (0, 1)
        sort_x(0)
        for i in range(12):
            hard[i] = stage.tile([P, 4 * W], F32, name="hard", tag="hard", bufs=3)
            for b in range(4):
                beam_bank(i, b)
                if i == 0 and b == 1:
                    group_wb(nc.vector.tensor_copy, 0, 0, 0, 256)
                    sort_rows()
                    turn_rows()
                    group_wb(nc.vector.tensor_copy, 0, 0, 256, W)
                    sort_x_codes(1)
                    quant_wb(0, 0, 0, W)
                    sort_x_scales(1)
                    nc.vector.tensor_copy(out=fac_sb[:], in_=fac_ps[:, 0 : AMP_ROW + 4, :])
                if i == 9 and b == 1:
                    gram_steps(range(2), [7])
                if i == 9 and b >= 2:
                    sin_bank((b - 2,), 0, both)
                if i == 10 and b == 0:
                    gram_steps([2], [6, 7])
                if i == 10 and b == 1:
                    sin_bank((2,), 0, both)
                    gram_open((3,), 0, both, ps_gram, "gram")
                    gram_steps([3], range(4, 8))
                if i == 10 and b == 3:
                    sin_bank((3,), 0, both)
                if i == 11 and b == 1:
                    gram_open((0, 1), 1, (0,), ps_gram, "gram")
                    gram_steps([0, 1], [8, 9])
            if i == 6:
                for j in range(3):
                    gram_open((j,), 0, both, ps_gram, "gram")
            if 6 <= i <= 8:
                gram_steps(range(3 if i < 8 else 2), [i - 2])
            if i == 1:
                group_wb(nc.scalar.copy, 1, 0, 0, 256)
            if i == 3:
                group_wb(nc.scalar.copy, 1, 0, 256, W)
            if i == 7:
                group_wb(nc.scalar.copy, 0, 1, 256, W)
            if i % 2:
                gp, first, rest = (0, GP_WORDS), (GP_WORDS, 256), (256, W)
            else:
                gp, first, rest = (W - GP_WORDS, W), (256, W - GP_WORDS), (0, 256)
            weigh(nc.gpsimd, fac_sb, i, *gp)
            weigh(nc.vector, fac_ps, i, *first)
            weigh(nc.vector, fac_ps, i, *rest)
            if i in (0, 1):
                sort_x(i + 2)
            if i in (2, 4):
                quant_wb(1, 0, 128 * (i - 2), 128 * i)
            if i in (3, 7):
                group_wb(nc.vector.tensor_copy, 1, 1, 64 * (i - 3), 64 * (i + 1))
            if i == 5:
                quant_wb(1, 1, 0, 256)
                group_wb(nc.vector.tensor_copy, 0, 1, 0, 256)
            if i == 6:
                quant_wb(0, 1, 0, 256)
            if i == 8:
                quant_wb(0, 1, 256, W)
                quant_wb(1, 1, 256, W)
            if i == 9:
                scale_unit(0, 0)
                scale_unit(1, 0)
            if i == 10:
                scale_unit(2, 0)
                round_unit(0, 0)
                scale_unit(3, 0)
            if i == 11:
                quant_u(i, 0, 256)
                quant_u(i, 256, W)
            else:
                quant_u(i)

        gram_open((2, 3), 1, (0,), ps_gram, "gram")
        gram_steps([2, 3], [8, 9])
        round_unit(1, 0, nc.scalar.copy)
        sin_bank((0, 1), 1, (0,))
        round_unit(2, 0, nc.scalar.copy)
        round_unit(3, 0, nc.scalar.copy)
        sin_bank((2, 3), 1, (0,))
        gram_open((0,), 1, (1,), ps_gram, "gram")
        gram_open((1,), 1, (1,), ps_beam, "beam")
        gram_open((2,), 1, (1,), ps_beam, "beam")
        gram_steps([0, 1, 2], [10])
        turn_units((0, 1), 0)
        copy_units((0, 1), 0)
        gram_open((3,), 1, (1,), ps_gram, "gram")
        gram_steps([3], [10])
        gram_pass(0, 11, 0)
        gram_pass(1, 11, 0)
        gram_pass(0, 11, 1)
        gram_pass(1, 11, 1)
        gram_steps([2, 3], [11])
        turn_units((2, 3), 0)
        for j in range(4):
            scale_unit(j, 1, (0,))
        round_unit(0, 1, cs=(0,))
        round_unit(1, 1, cs=(0,))
        for j in range(4):
            sin_bank((j,), 1, (1,))
        quant_units((0, 1), 0)
        scale_unit(0, 1, (1,))
        scale_unit(1, 1, (1,))
        round_unit(0, 1, cs=(1,))
        scale_unit(2, 1, (1,))
        round_unit(1, 1, cs=(1,))
        round_unit(2, 1, nc.scalar.copy, cs=(0,))
        round_unit(3, 1, nc.scalar.copy, cs=(0,))
        copy_units((2, 3), 0)
        scale_unit(3, 1, (1,))
        round_unit(2, 1, cs=(1,))
        round_unit(3, 1, cs=(1,))
        quant_units((2, 3), 0)
        store_codes(0, 0, NA, nc.sync)
        for j in range(4):
            turn_units((j,), 1)
            copy_units((j,), 1)
        for j in range(4):
            quant_units((j,), 1)
            if j == 2:
                store_codes(1, 0, 3 * P, nc.sync)
        store_codes(1, 3 * P, NA, nc.scalar)
        for q in range(4):
            store_scales(q, nc.sync if q < 2 else nc.scalar)
